import numpy as np
import ml_dtypes


def mxq(x, axis, fmt="e4m3"):
    dtype, down = {"e4m3": (ml_dtypes.float8_e4m3fn, 7), "e5m2": (ml_dtypes.float8_e5m2, 14)}[fmt]
    v = np.moveaxis(np.asarray(x, np.float32).astype(ml_dtypes.bfloat16).astype(np.float64), axis, -1)
    blocks = v.reshape(v.shape[:-1] + (-1, 32))
    amax = np.abs(blocks).max(-1, keepdims=True)
    byte = np.maximum(np.where(amax > 0, np.frexp(amax)[1] - 1 + 127, 0) - down, 1)
    scale = np.exp2(byte - 127.0)
    codes = (blocks / scale).astype(np.float32).astype(dtype).astype(np.float64)
    return np.moveaxis((codes * scale).reshape(v.shape), -1, axis)


WIDE = False


def mx_kscale(k):
    if not WIDE:
        return np.ones(k)
    levels = np.array([10, -10, 5, -5, 0])
    if k % 512:
        return np.exp2(np.random.permutation(np.resize(levels, k // 32))).repeat(32)
    a = np.empty((k // 512, 16))
    for p in range(k // 512):
        a[p, :8] = np.random.permutation(np.resize(levels, 8))
        for g in range(8):
            far = levels[np.abs(levels - a[p, g]) >= 10]
            a[p, g + 8] = far[np.random.randint(len(far))]
    return np.exp2(a.ravel()).repeat(32)


def f64(x):
    return np.asarray(x).astype(np.float64)


def striped(idx):
    return np.tile(np.asarray(idx).reshape(-1, 16).T, (8, 1)).astype(np.uint16)


def unstriped(offs):
    return offs[:16].T.reshape(-1).astype(np.int64)


E2M1 = np.array([0.0, 0.5, 1.0, 1.5, 2.0, 3.0, 4.0, 6.0, -0.0, -0.5, -1.0, -1.5, -2.0, -3.0, -4.0, -6.0])


def pack_weight(w, fmt):
    k, n = w.shape
    w = f64(np.asarray(w, np.float32).astype(ml_dtypes.bfloat16)).reshape(k // 32, 32, n)
    amax = np.abs(w).max(1)
    if fmt == "e4m3":
        byte = np.frexp(amax)[1] - 1 + 127 - 7
    else:
        mant, ex = np.frexp(amax / 6.0)
        byte = np.where(mant > 0.5, ex, ex - 1) + 127
    byte = np.clip(np.where(amax > 0, byte, 1), 1, 254)
    scaled = (w * np.exp2(127.0 - byte)[:, None, :]).reshape(k, n).astype(np.float32)
    by_word = np.ascontiguousarray(scaled.reshape(k // 512, 128, 4, n).transpose(0, 1, 3, 2))
    if fmt == "e4m3":
        words = by_word.astype(ml_dtypes.float8_e4m3fn).view(np.uint8)
    else:
        c = by_word.astype(ml_dtypes.float4_e2m1fn).view(np.uint8) & 0xF
        words = (c[..., 0::2] | (c[..., 1::2] << 4)).reshape(k // 512, 128, 2 * n)
    return np.ascontiguousarray(words), np.ascontiguousarray(byte.astype(np.uint8).reshape(k // 512, 16, n))


def unpack_weight(words, scales, fmt):
    g, _, n = scales.shape
    words = np.ascontiguousarray(words).reshape(g, 128, n, -1)
    if fmt == "e4m3":
        vals = words.view(ml_dtypes.float8_e4m3fn).astype(np.float64)
    else:
        nib = np.empty((g, 128, n, 4), np.uint8)
        nib[..., 0::2] = words & 0xF
        nib[..., 1::2] = words >> 4
        vals = E2M1[nib]
    vals = vals * np.repeat(np.exp2(scales.astype(np.float64) - 127.0), 8, axis=1)[..., None]
    return vals.transpose(0, 1, 3, 2).reshape(g * 512, n)


B, N, T, D, NQ = 1, 512, 2048, 512, 256


def setup_inputs():
    n = np.random.standard_normal
    idx = np.random.permutation(T)[:B * N]
    s = mx_kscale(D)[:, None]
    kp = pack_weight(n((D, T)) / s, "e4m3")
    return {
        "qT": (n((B, D, NQ)) * s * (3.00 / np.sqrt(D))).astype(np.float32),
        "k_words": kp[0],
        "k_scales": kp[1],
        "pr": np.tile(np.random.uniform(0.0, 4.0, 2048), (128, 1)).astype(np.float32),
        "pw": (np.random.uniform(0.1, 1.0, (B, NQ, 1))).astype(np.float32),
        "offs": striped(idx),
    }


def reference(qT, k_words, k_scales, pr, pw, offs):
    idx = unstriped(offs)
    pick = lambda x, which: x[:, which].reshape(x.shape[0], B, -1).transpose(1, 0, 2)
    k = unpack_weight(k_words, k_scales, "e4m3")
    kg = pick(k, idx)
    qq = mxq(f64(qT), 1, "e4m3")
    a = qq.transpose(0, 2, 1) @ kg
    y = 10.0 * np.tanh((a - f64(pw) * pick(f64(pr), idx)[:, :1, :]) / 10.0)
    return y

@@ -1,0 +1,120 @@
+from contextlib import ExitStack
+
+import concourse.mybir as mybir
+from concourse.masks import make_identity
+
+F32 = mybir.dt.float32
+BF16 = mybir.dt.bfloat16
+I32 = mybir.dt.int32
+U32 = mybir.dt.uint32
+U16 = mybir.dt.uint16
+U8 = mybir.dt.uint8
+FP8X4 = mybir.dt.float8_e4m3fn_x4
+ALU = mybir.AluOpType
+ACT = mybir.ActivationFunctionType
+
+P = 128
+D, NQ, T, N = 512, 256, 2048, 512
+PACK = 4
+TILES = NQ // P
+HALVES = 2
+NH = N // HALVES
+CAP = 10.0
+PRICE_ROW = 16
+
+FLOPS = 2 * D * NQ * N
+BYTES = 4 * D * NQ + D * T + 16 * T + 4 * T + 4 * NQ + 2 * N + 4 * NQ * N
+
+
+def tile_attend_link_budget_topk_kernel(tc, qT, k_words, k_scales, pr, pw, offs, out):
+    nc = tc.nc
+    with ExitStack() as ctx:
+        sb = ctx.enter_context(tc.tile_pool(name="sb", bufs=1))
+        ps = ctx.enter_context(tc.psum_pool(name="ps", bufs=1))
+
+        offsets = sb.tile([P, N // 16], U16, name="offsets")
+        nc.sync.dma_start(offsets[:], offs)
+        q_raw = sb.tile([P, PACK, NQ], F32, name="q_raw")
+        nc.sync.dma_start(q_raw[:], qT[0].rearrange("(p j) q -> p j q", j=PACK))
+        words = sb.tile([P, T], I32, name="words", align_bytes=64)
+        nc.sync.dma_start(words[:], k_words[0].rearrange("p t r -> p (t r)").bitcast(I32))
+
+        scales = sb.tile([P, T], U8, name="scales", align_bytes=64)
+        nc.vector.memset(scales[:].bitcast(I32), 0)
+        for quad in range(4):
+            nc.scalar.dma_start(
+                scales[32 * quad : 32 * quad + 4, :].bitcast(I32),
+                k_scales[0, 4 * quad : 4 * quad + 4, :].bitcast(I32),
+            )
+        prices = sb.tile([P, T], F32, name="prices", tag="shared", align_bytes=64)
+        nc.vector.memset(prices[:], 0.0)
+        nc.scalar.dma_start(prices[PRICE_ROW : PRICE_ROW + 1, :], pr[PRICE_ROW : PRICE_ROW + 1, :])
+
+        warm = sb.tile([P, 1], F32, name="warm")
+        nc.vector.memset(warm[:], 0.0)
+        nc.scalar.activation(warm[:], warm[:], ACT.Tanh)
+        weight = sb.tile([P, TILES], F32, name="weight")
+        nc.sync.dma_start(weight[:], pw[0].rearrange("(p t) o -> p (t o)", t=TILES))
+        ident = sb.tile([P, P], F32, name="ident")
+        make_identity(nc, ident[:])
+
+        g_scales = sb.tile([P, N], U8, name="g_scales", align_bytes=64)
+        nc.vector.tensor_copy(g_scales[:], scales[:].indirect(offsets[:]))
+
+        cols = NH // 16
+        blocks = NH // P
+        spread = []
+        for h in range(HALVES):
+            g_price = sb.tile([P, NH], F32, name=f"g_price{h}")
+            nc.vector.tensor_copy(g_price[:], prices[:].indirect(offsets[:, h * cols : (h + 1) * cols]))
+            turned = ps.tile([P, blocks, P], F32, name=f"turned{h}")
+            for c in range(blocks):
+                nc.tensor.transpose(turned[:, c, :], g_price[:, c * P : (c + 1) * P], ident[:])
+            column = sb.tile([P, blocks], F32, name=f"column{h}")
+            nc.scalar.copy(column[:], turned[:, :, PRICE_ROW])
+            wide = ps.tile([P, blocks, P], F32, name=f"wide{h}")
+            for c in range(blocks):
+                nc.tensor.transpose(wide[:, c, :], column[:, c : c + 1].to_broadcast([P, P]), ident[:])
+            price = sb.tile([P, NH], F32, name=f"price{h}")
+            nc.scalar.copy(price[:], wide[:].rearrange("p c n -> p (c n)"))
+            spread.append(price)
+
+        q_bf = sb.tile([P, TILES, P, PACK], BF16, name="q_bf", align_bytes=64)
+        nc.scalar.copy(
+            q_bf[:].rearrange("p t (a m) j -> p a t m j", m=2),
+            q_raw[:].rearrange("p j (a m t) -> p a t m j", m=2, t=TILES),
+        )
+        q_codes = sb.tile([P, NQ], U32, name="q_codes", align_bytes=64)
+        q_scales = sb.tile([P, NQ], U8, name="q_scales", align_bytes=64)
+        nc.vector.quantize_mx(
+            out=q_codes[:].bitcast(FP8X4),
+            scales=q_scales[:],
+            in_=q_bf[:].rearrange("p t m j -> p (t m j)"),
+        )
+
+        out_rows = out[0].rearrange("(p t) n -> p t n", t=TILES)
+        g_words = sb.tile([P, N], U32, name="g_words", tag="shared", align_bytes=64)
+        for h in range(HALVES):
+            nc.vector.tensor_copy(
+                g_words[:, h * NH : (h + 1) * NH], words[:].bitcast(U32).indirect(offsets[:, h * cols : (h + 1) * cols])
+            )
+            for t in range(TILES):
+                score = ps.tile([P, NH], F32, name=f"score{h}{t}")
+                nc.tensor.matmul_mx(
+                    out=score[:],
+                    lhsT=q_codes[:, t * P : (t + 1) * P].bitcast(FP8X4),
+                    lhsT_scale=q_scales[:, t * P : (t + 1) * P],
+                    rhs=g_words[:, h * NH : (h + 1) * NH].bitcast(FP8X4),
+                    rhs_scale=g_scales[:, h * NH : (h + 1) * NH],
+                    start=True,
+                    stop=True,
+                )
+                deficit = sb.tile([P, NH], F32, name=f"deficit{h}{t}")
+                nc.vector.scalar_tensor_tensor(
+                    deficit[:], spread[h][:], weight[:, t : t + 1], score[:], ALU.mult, ALU.subtract
+                )
+                capped = sb.tile([P, NH], F32, name=f"capped{h}{t}")
+                nc.scalar.activation(capped[:], deficit[:], ACT.Tanh, scale=-1.0 / CAP)
+                result = sb.tile([P, NH], F32, name=f"result{h}{t}")
+                nc.vector.tensor_scalar(result[:], capped[:], CAP, None, ALU.mult)
+                nc.sync.dma_start(out_rows[:, t, h * NH : (h + 1) * NH], result[:])

@@ -30,36 +30,35 @@ def tile_attend_link_budget_topk_kernel(tc, qT, k_words, k_scales, pr, pw, offs,
     nc = tc.nc
     with ExitStack() as ctx:
         sb = ctx.enter_context(tc.tile_pool(name="sb", bufs=1))
+        placed = ctx.enter_context(tc.tile_pool(name="placed", bufs=1))
         ps = ctx.enter_context(tc.psum_pool(name="ps", bufs=1))
 
         offsets = sb.tile([P, N // 16], U16, name="offsets")
         nc.sync.dma_start(offsets[:], offs)
         q_raw = sb.tile([P, PACK, NQ], F32, name="q_raw")
         nc.sync.dma_start(q_raw[:], qT[0].rearrange("(p j) q -> p j q", j=PACK))
-        words = sb.tile([P, T], I32, name="words", align_bytes=64)
-        nc.sync.dma_start(words[:], k_words[0].rearrange("p t r -> p (t r)").bitcast(I32))
+        weight = sb.tile([P, TILES], F32, name="weight")
+        nc.sync.dma_start(weight[:], pw[0].rearrange("(p t) o -> p (t o)", t=TILES))
 
+        prices = sb.tile([P, T], F32, name="prices", tag="prices", align_bytes=64)
+        nc.vector.memset(prices[:], 0.0)
+        nc.sync.dma_start(prices[PRICE_ROW : PRICE_ROW + 1, :], pr[PRICE_ROW : PRICE_ROW + 1, :])
         scales = sb.tile([P, T], U8, name="scales", align_bytes=64)
         nc.vector.memset(scales[:].bitcast(I32), 0)
         for quad in range(4):
-            nc.scalar.dma_start(
+            nc.sync.dma_start(
                 scales[32 * quad : 32 * quad + 4, :].bitcast(I32),
                 k_scales[0, 4 * quad : 4 * quad + 4, :].bitcast(I32),
             )
-        prices = sb.tile([P, T], F32, name="prices", tag="shared", align_bytes=64)
-        nc.vector.memset(prices[:], 0.0)
-        nc.scalar.dma_start(prices[PRICE_ROW : PRICE_ROW + 1, :], pr[PRICE_ROW : PRICE_ROW + 1, :])
-
+        warm_in = sb.tile([P, 1], F32, name="warm_in", tag="words", align_bytes=64)
+        nc.vector.memset(warm_in[:], 0.0)
         warm = sb.tile([P, 1], F32, name="warm")
-        nc.vector.memset(warm[:], 0.0)
-        nc.scalar.activation(warm[:], warm[:], ACT.Tanh)
-        weight = sb.tile([P, TILES], F32, name="weight")
-        nc.sync.dma_start(weight[:], pw[0].rearrange("(p t) o -> p (t o)", t=TILES))
+        nc.scalar.activation(warm[:], warm_in[:], ACT.Tanh)
+        words = sb.tile([P, T], I32, name="words", tag="words", align_bytes=64)
+        nc.sync.dma_start(words[:], k_words[0].rearrange("p t r -> p (t r)").bitcast(I32))
+
         ident = sb.tile([P, P], F32, name="ident")
         make_identity(nc, ident[:])
-
-        g_scales = sb.tile([P, N], U8, name="g_scales", align_bytes=64)
-        nc.vector.tensor_copy(g_scales[:], scales[:].indirect(offsets[:]))
 
         cols = NH // 16
         blocks = NH // P
@@ -70,7 +69,7 @@ def tile_attend_link_budget_topk_kernel(tc, qT, k_words, k_scales, pr, pw, offs,
             turned = ps.tile([P, blocks, P], F32, name=f"turned{h}")
             for c in range(blocks):
                 nc.tensor.transpose(turned[:, c, :], g_price[:, c * P : (c + 1) * P], ident[:])
-            column = sb.tile([P, blocks], F32, name=f"column{h}")
+            column = sb.tile([P, blocks], F32, name=f"column{h}", tag=f"column{h}", align_bytes=64)
             nc.scalar.copy(column[:], turned[:, :, PRICE_ROW])
             wide = ps.tile([P, blocks, P], F32, name=f"wide{h}")
             for c in range(blocks):
@@ -79,12 +78,15 @@ def tile_attend_link_budget_topk_kernel(tc, qT, k_words, k_scales, pr, pw, offs,
             nc.scalar.copy(price[:], wide[:].rearrange("p c n -> p (c n)"))
             spread.append(price)
 
-        q_bf = sb.tile([P, TILES, P, PACK], BF16, name="q_bf", align_bytes=64)
+        g_scales = sb.tile([P, N], U8, name="g_scales", tag="prices", align_bytes=64)
+        nc.vector.tensor_copy(g_scales[:], scales[:].indirect(offsets[:]))
+
+        q_bf = placed.tile([P, TILES, P, PACK], BF16, name="q_bf", align_bytes=64, offset=0)
         nc.scalar.copy(
             q_bf[:].rearrange("p t (a m) j -> p a t m j", m=2),
             q_raw[:].rearrange("p j (a m t) -> p a t m j", m=2, t=TILES),
         )
-        q_codes = sb.tile([P, NQ], U32, name="q_codes", align_bytes=64)
+        q_codes = sb.tile([P, NQ], U32, name="q_codes", tag="column0", align_bytes=64)
         q_scales = sb.tile([P, NQ], U8, name="q_scales", align_bytes=64)
         nc.vector.quantize_mx(
             out=q_codes[:].bitcast(FP8X4),
@@ -93,10 +95,10 @@ def tile_attend_link_budget_topk_kernel(tc, qT, k_words, k_scales, pr, pw, offs,
         )
 
         out_rows = out[0].rearrange("(p t) n -> p t n", t=TILES)
-        g_words = sb.tile([P, N], U32, name="g_words", tag="shared", align_bytes=64)
         for h in range(HALVES):
+            g_words = placed.tile([P, NH], U32, name=f"g_words{h}", align_bytes=64, offset=4 * NH * h)
             nc.vector.tensor_copy(
-                g_words[:, h * NH : (h + 1) * NH], words[:].bitcast(U32).indirect(offsets[:, h * cols : (h + 1) * cols])
+                g_words[:], words[:].bitcast(U32).indirect(offsets[:, h * cols : (h + 1) * cols])
             )
             for t in range(TILES):
                 score = ps.tile([P, NH], F32, name=f"score{h}{t}")
@@ -104,7 +106,7 @@ def tile_attend_link_budget_topk_kernel(tc, qT, k_words, k_scales, pr, pw, offs,
                     out=score[:],
                     lhsT=q_codes[:, t * P : (t + 1) * P].bitcast(FP8X4),
                     lhsT_scale=q_scales[:, t * P : (t + 1) * P],
-                    rhs=g_words[:, h * NH : (h + 1) * NH].bitcast(FP8X4),
+                    rhs=g_words[:].bitcast(FP8X4),
                     rhs_scale=g_scales[:, h * NH : (h + 1) * NH],
                     start=True,
                     stop=True,

@@ -30,17 +30,14 @@ def tile_attend_link_budget_topk_kernel(tc, qT, k_words, k_scales, pr, pw, offs,
     nc = tc.nc
     with ExitStack() as ctx:
         sb = ctx.enter_context(tc.tile_pool(name="sb", bufs=1))
-        placed = ctx.enter_context(tc.tile_pool(name="placed", bufs=1))
         ps = ctx.enter_context(tc.psum_pool(name="ps", bufs=1))
 
         offsets = sb.tile([P, N // 16], U16, name="offsets")
         nc.sync.dma_start(offsets[:], offs)
         q_raw = sb.tile([P, PACK, NQ], F32, name="q_raw")
         nc.sync.dma_start(q_raw[:], qT[0].rearrange("(p j) q -> p j q", j=PACK))
-        weight = sb.tile([P, TILES], F32, name="weight")
-        nc.sync.dma_start(weight[:], pw[0].rearrange("(p t) o -> p (t o)", t=TILES))
 
-        prices = sb.tile([P, T], F32, name="prices", tag="prices", align_bytes=64)
+        prices = sb.tile([P, T], F32, name="prices")
         nc.vector.memset(prices[:], 0.0)
         nc.sync.dma_start(prices[PRICE_ROW : PRICE_ROW + 1, :], pr[PRICE_ROW : PRICE_ROW + 1, :])
         scales = sb.tile([P, T], U8, name="scales", align_bytes=64)
@@ -52,41 +49,44 @@ def tile_attend_link_budget_topk_kernel(tc, qT, k_words, k_scales, pr, pw, offs,
             )
         warm_in = sb.tile([P, 1], F32, name="warm_in", tag="words", align_bytes=64)
         nc.vector.memset(warm_in[:], 0.0)
-        warm = sb.tile([P, 1], F32, name="warm")
+        warm = sb.tile([P, 1], F32, name="warm", tag="weight")
         nc.scalar.activation(warm[:], warm_in[:], ACT.Tanh)
         words = sb.tile([P, T], I32, name="words", tag="words", align_bytes=64)
         nc.sync.dma_start(words[:], k_words[0].rearrange("p t r -> p (t r)").bitcast(I32))
 
+        weight = sb.tile([P, TILES], F32, name="weight", tag="weight")
+        nc.sync.dma_start(weight[:], pw[0].rearrange("(p t) o -> p (t o)", t=TILES))
         ident = sb.tile([P, P], F32, name="ident")
-        make_identity(nc, ident[:])
+        nc.vector.memset(ident[:], 0.0)
+        make_identity(nc, ident[:], nomemset=True)
 
         cols = NH // 16
         blocks = NH // P
         spread = []
         for h in range(HALVES):
-            g_price = sb.tile([P, NH], F32, name=f"g_price{h}")
+            g_price = sb.tile([P, NH], F32, name=f"g_price{h}", tag=f"g_price{h}", align_bytes=64)
             nc.vector.tensor_copy(g_price[:], prices[:].indirect(offsets[:, h * cols : (h + 1) * cols]))
-            turned = ps.tile([P, blocks, P], F32, name=f"turned{h}")
+            turned = ps.tile([P, blocks, P], F32, name=f"turned{h}", tag=f"turned{h}")
             for c in range(blocks):
                 nc.tensor.transpose(turned[:, c, :], g_price[:, c * P : (c + 1) * P], ident[:])
             column = sb.tile([P, blocks], F32, name=f"column{h}", tag=f"column{h}", align_bytes=64)
             nc.scalar.copy(column[:], turned[:, :, PRICE_ROW])
-            wide = ps.tile([P, blocks, P], F32, name=f"wide{h}")
+            wide = ps.tile([P, blocks, P], F32, name=f"wide{h}", tag=f"wide{h}")
             for c in range(blocks):
                 nc.tensor.transpose(wide[:, c, :], column[:, c : c + 1].to_broadcast([P, P]), ident[:])
             price = sb.tile([P, NH], F32, name=f"price{h}")
             nc.scalar.copy(price[:], wide[:].rearrange("p c n -> p (c n)"))
             spread.append(price)
 
-        g_scales = sb.tile([P, N], U8, name="g_scales", tag="prices", align_bytes=64)
+        g_scales = sb.tile([P, N], U8, name="g_scales", align_bytes=64)
         nc.vector.tensor_copy(g_scales[:], scales[:].indirect(offsets[:]))
 
-        q_bf = placed.tile([P, TILES, P, PACK], BF16, name="q_bf", align_bytes=64, offset=0)
+        q_bf = sb.tile([P, TILES, P, PACK], BF16, name="q_bf", align_bytes=64)
         nc.scalar.copy(
             q_bf[:].rearrange("p t (a m) j -> p a t m j", m=2),
             q_raw[:].rearrange("p j (a m t) -> p a t m j", m=2, t=TILES),
         )
-        q_codes = sb.tile([P, NQ], U32, name="q_codes", tag="column0", align_bytes=64)
+        q_codes = sb.tile([P, NQ], U32, name="q_codes", tag="g_price0", align_bytes=64)
         q_scales = sb.tile([P, NQ], U8, name="q_scales", align_bytes=64)
         nc.vector.quantize_mx(
             out=q_codes[:].bitcast(FP8X4),
@@ -95,28 +95,34 @@ def tile_attend_link_budget_topk_kernel(tc, qT, k_words, k_scales, pr, pw, offs,
         )
 
         out_rows = out[0].rearrange("(p t) n -> p t n", t=TILES)
-        for h in range(HALVES):
-            g_words = placed.tile([P, NH], U32, name=f"g_words{h}", align_bytes=64, offset=4 * NH * h)
-            nc.vector.tensor_copy(
-                g_words[:], words[:].bitcast(U32).indirect(offsets[:, h * cols : (h + 1) * cols])
+        gathered = []
+        pieces = [(0, 0, 0, NH), (0, 1, 0, NH), (1, 0, 0, NH), (1, 1, 0, NH)]
+        banks = ["turned1", "wide0", "turned0", "wide1"]
+        for i, (h, t, lo, hi) in enumerate(pieces):
+            if h == len(gathered):
+                g_words = sb.tile([P, NH], U32, name=f"g_words{h}", tag=("g_words0", "column1")[h], align_bytes=64)
+                nc.vector.tensor_copy(
+                    g_words[:], words[:].bitcast(U32).indirect(offsets[:, h * cols : (h + 1) * cols])
+                )
+                gathered.append(g_words)
+            width = hi - lo
+            slots = slice(h * NH + lo, h * NH + hi)
+            score = ps.tile([P, width], F32, name=f"score{i}", tag=banks[i])
+            nc.tensor.matmul_mx(
+                out=score[:],
+                lhsT=q_codes[:, t * P : (t + 1) * P].bitcast(FP8X4),
+                lhsT_scale=q_scales[:, t * P : (t + 1) * P],
+                rhs=gathered[h][:, lo:hi].bitcast(FP8X4),
+                rhs_scale=g_scales[:, slots],
+                start=True,
+                stop=True,
             )
-            for t in range(TILES):
-                score = ps.tile([P, NH], F32, name=f"score{h}{t}")
-                nc.tensor.matmul_mx(
-                    out=score[:],
-                    lhsT=q_codes[:, t * P : (t + 1) * P].bitcast(FP8X4),
-                    lhsT_scale=q_scales[:, t * P : (t + 1) * P],
-                    rhs=g_words[:].bitcast(FP8X4),
-                    rhs_scale=g_scales[:, h * NH : (h + 1) * NH],
-                    start=True,
-                    stop=True,
-                )
-                deficit = sb.tile([P, NH], F32, name=f"deficit{h}{t}")
-                nc.vector.scalar_tensor_tensor(
-                    deficit[:], spread[h][:], weight[:, t : t + 1], score[:], ALU.mult, ALU.subtract
-                )
-                capped = sb.tile([P, NH], F32, name=f"capped{h}{t}")
-                nc.scalar.activation(capped[:], deficit[:], ACT.Tanh, scale=-1.0 / CAP)
-                result = sb.tile([P, NH], F32, name=f"result{h}{t}")
-                nc.vector.tensor_scalar(result[:], capped[:], CAP, None, ALU.mult)
-                nc.sync.dma_start(out_rows[:, t, h * NH : (h + 1) * NH], result[:])
+            deficit = sb.tile([P, width], F32, name=f"deficit{i}")
+            nc.vector.scalar_tensor_tensor(
+                deficit[:], spread[h][:, lo:hi], weight[:, t : t + 1], score[:], ALU.mult, ALU.subtract
+            )
+            capped = sb.tile([P, width], F32, name=f"capped{i}")
+            nc.scalar.activation(capped[:], deficit[:], ACT.Tanh, scale=-1.0 / CAP)
+            result = sb.tile([P, width], F32, name=f"result{i}")
+            nc.vector.tensor_scalar(result[:], capped[:], CAP, None, ALU.mult)
+            nc.sync.dma_start(out_rows[:, t, slots], result[:])

@@ -20,7 +20,7 @@ TILES = NQ // P
 HALVES = 2
 NH = N // HALVES
 CAP = 10.0
-PRICE_ROW = 16
+PRICE_ROW = P - 1
 
 FLOPS = 2 * D * NQ * N
 BYTES = 4 * D * NQ + D * T + 16 * T + 4 * T + 4 * NQ + 2 * N + 4 * NQ * N
@@ -34,31 +34,22 @@ def tile_attend_link_budget_topk_kernel(tc, qT, k_words, k_scales, pr, pw, offs,
 
         offsets = sb.tile([P, N // 16], U16, name="offsets")
         nc.sync.dma_start(offsets[:], offs)
-        q_raw = sb.tile([P, PACK, NQ], F32, name="q_raw")
-        nc.sync.dma_start(q_raw[:], qT[0].rearrange("(p j) q -> p j q", j=PACK))
-
-        prices = sb.tile([P, T], F32, name="prices")
-        nc.vector.memset(prices[:], 0.0)
-        nc.sync.dma_start(prices[PRICE_ROW : PRICE_ROW + 1, :], pr[PRICE_ROW : PRICE_ROW + 1, :])
         scales = sb.tile([P, T], U8, name="scales", align_bytes=64)
         nc.vector.memset(scales[:].bitcast(I32), 0)
-        for quad in range(4):
-            nc.sync.dma_start(
-                scales[32 * quad : 32 * quad + 4, :].bitcast(I32),
-                k_scales[0, 4 * quad : 4 * quad + 4, :].bitcast(I32),
-            )
-        warm_in = sb.tile([P, 1], F32, name="warm_in", tag="words", align_bytes=64)
-        nc.vector.memset(warm_in[:], 0.0)
-        warm = sb.tile([P, 1], F32, name="warm", tag="weight")
-        nc.scalar.activation(warm[:], warm_in[:], ACT.Tanh)
-        words = sb.tile([P, T], I32, name="words", tag="words", align_bytes=64)
-        nc.sync.dma_start(words[:], k_words[0].rearrange("p t r -> p (t r)").bitcast(I32))
-
-        weight = sb.tile([P, TILES], F32, name="weight", tag="weight")
-        nc.sync.dma_start(weight[:], pw[0].rearrange("(p t) o -> p (t o)", t=TILES))
         ident = sb.tile([P, P], F32, name="ident")
         nc.vector.memset(ident[:], 0.0)
         make_identity(nc, ident[:], nomemset=True)
+        prices = sb.tile([P, T], F32, name="prices")
+        nc.vector.memset(prices[:PRICE_ROW, :], 0.0)
+        nc.sync.dma_start(prices[PRICE_ROW:, :], pr[PRICE_ROW:, :])
+        q_raw = sb.tile([P, PACK, NQ], F32, name="q_raw")
+        nc.sync.dma_start(q_raw[:], qT[0].rearrange("(p j) q -> p j q", j=PACK))
+        for f in range(4):
+            nc.sync.dma_start(scales[f:P:32, :].bitcast(I32), k_scales[0, f:16:4, :].bitcast(I32))
+        words = sb.tile([P, T], I32, name="words", align_bytes=64)
+        nc.sync.dma_start(words[:], k_words[0].rearrange("p t r -> p (t r)").bitcast(I32))
+        weight = sb.tile([P, TILES], F32, name="weight")
+        nc.sync.dma_start(weight[:], pw[0].rearrange("(p t) o -> p (t o)", t=TILES))
 
         cols = NH // 16
         blocks = NH // P

@@ -1,7 +1,6 @@
 from contextlib import ExitStack
 
 import concourse.mybir as mybir
-from concourse.masks import make_identity
 
 F32 = mybir.dt.float32
 BF16 = mybir.dt.bfloat16
@@ -21,6 +20,8 @@ HALVES = 2
 NH = N // HALVES
 CAP = 10.0
 PRICE_ROW = P - 1
+WORDS_AT = 4 * NQ + 4 * N
+WEIGHT_AT = WORDS_AT + 4 * T
 
 FLOPS = 2 * D * NQ * N
 BYTES = 4 * D * NQ + D * T + 16 * T + 4 * T + 4 * NQ + 2 * N + 4 * NQ * N
@@ -30,38 +31,56 @@ def tile_attend_link_budget_topk_kernel(tc, qT, k_words, k_scales, pr, pw, offs,
     nc = tc.nc
     with ExitStack() as ctx:
         sb = ctx.enter_context(tc.tile_pool(name="sb", bufs=1))
+        placed = ctx.enter_context(tc.tile_pool(name="placed", bufs=1))
         ps = ctx.enter_context(tc.psum_pool(name="ps", bufs=1))
 
         offsets = sb.tile([P, N // 16], U16, name="offsets")
         nc.sync.dma_start(offsets[:], offs)
-        scales = sb.tile([P, T], U8, name="scales", align_bytes=64)
-        nc.vector.memset(scales[:].bitcast(I32), 0)
+        scales = placed.tile([P, T], U8, name="scales", align_bytes=64, offset=0)
+        nc.gpsimd.memset(scales[:].bitcast(I32), 0)
+        zeros = placed.tile([P, P], F32, name="zeros", align_bytes=64, offset=WEIGHT_AT - 2 * P)
+        nc.gpsimd.memset(zeros[:], 0.0)
         ident = sb.tile([P, P], F32, name="ident")
-        nc.vector.memset(ident[:], 0.0)
-        make_identity(nc, ident[:], nomemset=True)
+        nc.gpsimd.affine_select(
+            out=ident[:],
+            in_=zeros[:],
+            compare_op=ALU.not_equal,
+            fill=1.0,
+            base=0,
+            pattern=[[-1, P]],
+            channel_multiplier=1,
+        )
         prices = sb.tile([P, T], F32, name="prices")
-        nc.vector.memset(prices[:PRICE_ROW, :], 0.0)
+        nc.vector.memset(prices[:PRICE_ROW, : T // 2 - 1], 0.0)
+        nc.vector.memset(prices[:PRICE_ROW, T // 2 - 1 :], 0.0)
         nc.sync.dma_start(prices[PRICE_ROW:, :], pr[PRICE_ROW:, :])
-        q_raw = sb.tile([P, PACK, NQ], F32, name="q_raw")
+        q_raw = sb.tile([P, PACK, NQ], F32, name="q_raw", tag="q_raw")
         nc.sync.dma_start(q_raw[:], qT[0].rearrange("(p j) q -> p j q", j=PACK))
         for f in range(4):
             nc.sync.dma_start(scales[f:P:32, :].bitcast(I32), k_scales[0, f:16:4, :].bitcast(I32))
-        words = sb.tile([P, T], I32, name="words", align_bytes=64)
+        words = placed.tile([P, T], I32, name="words", align_bytes=64, offset=WORDS_AT)
         nc.sync.dma_start(words[:], k_words[0].rearrange("p t r -> p (t r)").bitcast(I32))
-        weight = sb.tile([P, TILES], F32, name="weight")
+        weight = placed.tile([P, TILES], F32, name="weight", align_bytes=64, offset=WEIGHT_AT)
         nc.sync.dma_start(weight[:], pw[0].rearrange("(p t) o -> p (t o)", t=TILES))
+
+        q_bf = sb.tile([P, TILES, P, PACK], BF16, name="q_bf", align_bytes=64)
+        nc.scalar.copy(
+            q_bf[:].rearrange("p t (a m) j -> p a t m j", m=2),
+            q_raw[:].rearrange("p j (a m t) -> p a t m j", m=2, t=TILES),
+        )
 
         cols = NH // 16
         blocks = NH // P
+        columns = sb.tile([P, HALVES, blocks], F32, name="columns", tag="q_raw")
         spread = []
         for h in range(HALVES):
-            g_price = sb.tile([P, NH], F32, name=f"g_price{h}", tag=f"g_price{h}", align_bytes=64)
+            g_price = sb.tile([P, NH], F32, name=f"g_price{h}", align_bytes=64)
             nc.vector.tensor_copy(g_price[:], prices[:].indirect(offsets[:, h * cols : (h + 1) * cols]))
             turned = ps.tile([P, blocks, P], F32, name=f"turned{h}", tag=f"turned{h}")
             for c in range(blocks):
                 nc.tensor.transpose(turned[:, c, :], g_price[:, c * P : (c + 1) * P], ident[:])
-            column = sb.tile([P, blocks], F32, name=f"column{h}", tag=f"column{h}", align_bytes=64)
-            nc.scalar.copy(column[:], turned[:, :, PRICE_ROW])
+            column = columns[:, h, :]
+            nc.scalar.copy(column, turned[:, :, PRICE_ROW])
             wide = ps.tile([P, blocks, P], F32, name=f"wide{h}", tag=f"wide{h}")
             for c in range(blocks):
                 nc.tensor.transpose(wide[:, c, :], column[:, c : c + 1].to_broadcast([P, P]), ident[:])
@@ -72,12 +91,7 @@ def tile_attend_link_budget_topk_kernel(tc, qT, k_words, k_scales, pr, pw, offs,
         g_scales = sb.tile([P, N], U8, name="g_scales", align_bytes=64)
         nc.vector.tensor_copy(g_scales[:], scales[:].indirect(offsets[:]))
 
-        q_bf = sb.tile([P, TILES, P, PACK], BF16, name="q_bf", align_bytes=64)
-        nc.scalar.copy(
-            q_bf[:].rearrange("p t (a m) j -> p a t m j", m=2),
-            q_raw[:].rearrange("p j (a m t) -> p a t m j", m=2, t=TILES),
-        )
-        q_codes = sb.tile([P, NQ], U32, name="q_codes", tag="g_price0", align_bytes=64)
+        q_codes = placed.tile([P, NQ], U32, name="q_codes", align_bytes=64, offset=0)
         q_scales = sb.tile([P, NQ], U8, name="q_scales", align_bytes=64)
         nc.vector.quantize_mx(
             out=q_codes[:].bitcast(FP8X4),
@@ -85,35 +99,49 @@ def tile_attend_link_budget_topk_kernel(tc, qT, k_words, k_scales, pr, pw, offs,
             in_=q_bf[:].rearrange("p t m j -> p (t m j)"),
         )
 
+        g_words = placed.tile([P, N], U32, name="g_words", align_bytes=64, offset=4 * NQ)
+        for h in range(HALVES):
+            nc.vector.tensor_copy(
+                g_words[:, h * NH : (h + 1) * NH],
+                words[:].bitcast(U32).indirect(offsets[:, h * cols : (h + 1) * cols]),
+            )
+
         out_rows = out[0].rearrange("(p t) n -> p t n", t=TILES)
-        gathered = []
-        pieces = [(0, 0, 0, NH), (0, 1, 0, NH), (1, 0, 0, NH), (1, 1, 0, NH)]
-        banks = ["turned1", "wide0", "turned0", "wide1"]
-        for i, (h, t, lo, hi) in enumerate(pieces):
-            if h == len(gathered):
-                g_words = sb.tile([P, NH], U32, name=f"g_words{h}", tag=("g_words0", "column1")[h], align_bytes=64)
-                nc.vector.tensor_copy(
-                    g_words[:], words[:].bitcast(U32).indirect(offsets[:, h * cols : (h + 1) * cols])
-                )
-                gathered.append(g_words)
-            width = hi - lo
-            slots = slice(h * NH + lo, h * NH + hi)
-            score = ps.tile([P, width], F32, name=f"score{i}", tag=banks[i])
-            nc.tensor.matmul_mx(
-                out=score[:],
-                lhsT=q_codes[:, t * P : (t + 1) * P].bitcast(FP8X4),
-                lhsT_scale=q_scales[:, t * P : (t + 1) * P],
-                rhs=gathered[h][:, lo:hi].bitcast(FP8X4),
-                rhs_scale=g_scales[:, slots],
-                start=True,
-                stop=True,
-            )
-            deficit = sb.tile([P, width], F32, name=f"deficit{i}")
-            nc.vector.scalar_tensor_tensor(
-                deficit[:], spread[h][:, lo:hi], weight[:, t : t + 1], score[:], ALU.mult, ALU.subtract
-            )
-            capped = sb.tile([P, width], F32, name=f"capped{i}")
-            nc.scalar.activation(capped[:], deficit[:], ACT.Tanh, scale=-1.0 / CAP)
-            result = sb.tile([P, width], F32, name=f"result{i}")
-            nc.vector.tensor_scalar(result[:], capped[:], CAP, None, ALU.mult)
+        capped = [sb.tile([P, N], F32, name=f"capped{t}") for t in range(TILES)]
+
+        def finish(t, slots):
+            result = sb.tile([P, slots.stop - slots.start], F32, name=f"result{t}_{slots.start}")
+            nc.vector.tensor_scalar(result[:], capped[t][:, slots], CAP, None, ALU.mult)
             nc.sync.dma_start(out_rows[:, t, slots], result[:])
+
+        banks = ["score0", "score1", "score2", "score3", "turned0", "turned1", "wide0", "wide1"]
+        for h in range(HALVES):
+            for t in range(TILES):
+                last = (h, t) in ((0, 0), (HALVES - 1, TILES - 1))
+                for c in range(blocks):
+                    slots = slice(h * NH + c * P, h * NH + (c + 1) * P)
+                    i = (h * TILES + t) * blocks + c
+                    score = ps.tile([P, P], F32, name=f"score{i}", tag=banks[i])
+                    nc.tensor.matmul_mx(
+                        out=score[:],
+                        lhsT=q_codes[:, t * P : (t + 1) * P].bitcast(FP8X4),
+                        lhsT_scale=q_scales[:, t * P : (t + 1) * P],
+                        rhs=g_words[:, slots].bitcast(FP8X4),
+                        rhs_scale=g_scales[:, slots],
+                        start=True,
+                        stop=True,
+                    )
+                    deficit = sb.tile([P, P], F32, name=f"deficit{i}")
+                    nc.vector.scalar_tensor_tensor(
+                        deficit[:],
+                        spread[h][:, c * P : (c + 1) * P],
+                        weight[:, t : t + 1],
+                        score[:],
+                        ALU.mult,
+                        ALU.subtract,
+                    )
+                    nc.scalar.activation(capped[t][:, slots], deficit[:], ACT.Tanh, scale=-1.0 / CAP)
+                    if last:
+                        finish(t, slots)
+                if not last:
+                    finish(t, slice(h * NH, (h + 1) * NH))

@@ -20,6 +20,7 @@ HALVES = 2
 NH = N // HALVES
 CAP = 10.0
 PRICE_ROW = P - 1
+CLEAR_V = 1280
 WORDS_AT = 4 * NQ + 4 * N
 WEIGHT_AT = WORDS_AT + 4 * T
 
@@ -37,7 +38,9 @@ def tile_attend_link_budget_topk_kernel(tc, qT, k_words, k_scales, pr, pw, offs,
         offsets = sb.tile([P, N // 16], U16, name="offsets")
         nc.sync.dma_start(offsets[:], offs)
         scales = placed.tile([P, T], U8, name="scales", align_bytes=64, offset=0)
-        nc.gpsimd.memset(scales[:].bitcast(I32), 0)
+        scale_words = scales[:].bitcast(I32)
+        nc.vector.memset(scale_words[:, : T // 8 - 1], 0)
+        nc.vector.memset(scale_words[:, T // 8 - 1 :], 0)
         zeros = placed.tile([P, P], F32, name="zeros", align_bytes=64, offset=WEIGHT_AT - 2 * P)
         nc.gpsimd.memset(zeros[:], 0.0)
         ident = sb.tile([P, P], F32, name="ident")
@@ -51,13 +54,14 @@ def tile_attend_link_budget_topk_kernel(tc, qT, k_words, k_scales, pr, pw, offs,
             channel_multiplier=1,
         )
         prices = sb.tile([P, T], F32, name="prices")
-        nc.vector.memset(prices[:PRICE_ROW, : T // 2 - 1], 0.0)
-        nc.vector.memset(prices[:PRICE_ROW, T // 2 - 1 :], 0.0)
-        nc.sync.dma_start(prices[PRICE_ROW:, :], pr[PRICE_ROW:, :])
+        nc.vector.memset(prices[:PRICE_ROW, : CLEAR_V // 2 - 1], 0.0)
+        nc.vector.memset(prices[:PRICE_ROW, CLEAR_V // 2 - 1 : CLEAR_V], 0.0)
+        nc.gpsimd.memset(prices[:PRICE_ROW, CLEAR_V:], 0.0)
+        nc.scalar.dma_start(prices[PRICE_ROW:, :], pr[PRICE_ROW:, :])
         q_raw = sb.tile([P, PACK, NQ], F32, name="q_raw", tag="q_raw")
         nc.sync.dma_start(q_raw[:], qT[0].rearrange("(p j) q -> p j q", j=PACK))
         for f in range(4):
-            nc.sync.dma_start(scales[f:P:32, :].bitcast(I32), k_scales[0, f:16:4, :].bitcast(I32))
+            nc.scalar.dma_start(scales[f:P:32, :].bitcast(I32), k_scales[0, f:16:4, :].bitcast(I32))
         words = placed.tile([P, T], I32, name="words", align_bytes=64, offset=WORDS_AT)
         nc.sync.dma_start(words[:], k_words[0].rearrange("p t r -> p (t r)").bitcast(I32))
         weight = placed.tile([P, TILES], F32, name="weight", align_bytes=64, offset=WEIGHT_AT)

@@ -20,9 +20,12 @@ HALVES = 2
 NH = N // HALVES
 CAP = 10.0
 PRICE_ROW = P - 1
-CLEAR_V = 1280
-WORDS_AT = 4 * NQ + 4 * N
+CLEAR_V = 640
+SCALE_ROW = 48
+PRICES_AT = T
+WORDS_AT = PRICES_AT + 4 * T
 WEIGHT_AT = WORDS_AT + 4 * T
+PLANE_AT = WEIGHT_AT + 64
 
 FLOPS = 2 * D * NQ * N
 BYTES = 4 * D * NQ + D * T + 16 * T + 4 * T + 4 * NQ + 2 * N + 4 * NQ * N
@@ -39,8 +42,10 @@ def tile_attend_link_budget_topk_kernel(tc, qT, k_words, k_scales, pr, pw, offs,
         nc.sync.dma_start(offsets[:], offs)
         scales = placed.tile([P, T], U8, name="scales", align_bytes=64, offset=0)
         scale_words = scales[:].bitcast(I32)
-        nc.vector.memset(scale_words[:, : T // 8 - 1], 0)
-        nc.vector.memset(scale_words[:, T // 8 - 1 :], 0)
+        for rows in (slice(0, SCALE_ROW), slice(SCALE_ROW + 16, P)):
+            nc.vector.memset(scale_words[rows, : T // 8 - 1], 0)
+            nc.vector.memset(scale_words[rows, T // 8 - 1 :], 0)
+        nc.scalar.dma_start(scale_words[SCALE_ROW : SCALE_ROW + 16, :], k_scales[0].bitcast(I32))
         zeros = placed.tile([P, P], F32, name="zeros", align_bytes=64, offset=WEIGHT_AT - 2 * P)
         nc.gpsimd.memset(zeros[:], 0.0)
         ident = sb.tile([P, P], F32, name="ident")
@@ -53,19 +58,28 @@ def tile_attend_link_budget_topk_kernel(tc, qT, k_words, k_scales, pr, pw, offs,
             pattern=[[-1, P]],
             channel_multiplier=1,
         )
-        prices = sb.tile([P, T], F32, name="prices")
+        prices = placed.tile([P, T], F32, name="prices", align_bytes=64, offset=PRICES_AT)
         nc.vector.memset(prices[:PRICE_ROW, : CLEAR_V // 2 - 1], 0.0)
         nc.vector.memset(prices[:PRICE_ROW, CLEAR_V // 2 - 1 : CLEAR_V], 0.0)
-        nc.gpsimd.memset(prices[:PRICE_ROW, CLEAR_V:], 0.0)
+        nc.gpsimd.memset(prices[:PRICE_ROW, CLEAR_V : CLEAR_V + P], 0.0)
+        nc.gpsimd.memset(prices[:PRICE_ROW, CLEAR_V + P :], 0.0)
         nc.scalar.dma_start(prices[PRICE_ROW:, :], pr[PRICE_ROW:, :])
         q_raw = sb.tile([P, PACK, NQ], F32, name="q_raw", tag="q_raw")
         nc.sync.dma_start(q_raw[:], qT[0].rearrange("(p j) q -> p j q", j=PACK))
-        for f in range(4):
-            nc.scalar.dma_start(scales[f:P:32, :].bitcast(I32), k_scales[0, f:16:4, :].bitcast(I32))
         words = placed.tile([P, T], I32, name="words", align_bytes=64, offset=WORDS_AT)
         nc.sync.dma_start(words[:], k_words[0].rearrange("p t r -> p (t r)").bitcast(I32))
         weight = placed.tile([P, TILES], F32, name="weight", align_bytes=64, offset=WEIGHT_AT)
         nc.sync.dma_start(weight[:], pw[0].rearrange("(p t) o -> p (t o)", t=TILES))
+
+        g_rows = sb.tile([P, N], U8, name="g_rows", align_bytes=64)
+        nc.vector.tensor_copy(g_rows[:], scales[:].indirect(offsets[:]))
+        g_scales = placed.tile([P, N], U8, name="g_scales", align_bytes=64, offset=PLANE_AT)
+        for quad in range(4):
+            first = SCALE_ROW + 4 * quad
+            nc.sync.dma_start(
+                g_scales[32 * quad : 32 * quad + 4, :].bitcast(I32),
+                g_rows[first : first + 4, :].bitcast(I32),
+            )
 
         q_bf = sb.tile([P, TILES, P, PACK], BF16, name="q_bf", align_bytes=64)
         nc.scalar.copy(
@@ -92,10 +106,8 @@ def tile_attend_link_budget_topk_kernel(tc, qT, k_words, k_scales, pr, pw, offs,
             nc.scalar.copy(price[:], wide[:].rearrange("p c n -> p (c n)"))
             spread.append(price)
 
-        g_scales = sb.tile([P, N], U8, name="g_scales", align_bytes=64)
-        nc.vector.tensor_copy(g_scales[:], scales[:].indirect(offsets[:]))
 
-        q_codes = placed.tile([P, NQ], U32, name="q_codes", align_bytes=64, offset=0)
+        q_codes = placed.tile([P, NQ], U32, name="q_codes", align_bytes=64, offset=PRICES_AT)
         q_scales = sb.tile([P, NQ], U8, name="q_scales", align_bytes=64)
         nc.vector.quantize_mx(
             out=q_codes[:].bitcast(FP8X4),
@@ -103,7 +115,7 @@ def tile_attend_link_budget_topk_kernel(tc, qT, k_words, k_scales, pr, pw, offs,
             in_=q_bf[:].rearrange("p t m j -> p (t m j)"),
         )
 
-        g_words = placed.tile([P, N], U32, name="g_words", align_bytes=64, offset=4 * NQ)
+        g_words = placed.tile([P, N], U32, name="g_words", align_bytes=64, offset=0)
         for h in range(HALVES):
             nc.vector.tensor_copy(
                 g_words[:, h * NH : (h + 1) * NH],

@@ -127,7 +127,10 @@ def tile_attend_link_budget_topk_kernel(tc, qT, k_words, k_scales, pr, pw, offs,
 
         def finish(t, slots):
             result = sb.tile([P, slots.stop - slots.start], F32, name=f"result{t}_{slots.start}")
-            nc.vector.tensor_scalar(result[:], capped[t][:, slots], CAP, None, ALU.mult)
+            if t == 0 and slots.start == 0:
+                nc.gpsimd.tensor_scalar(result[:], capped[t][:, slots], CAP, 0.0, ALU.mult, ALU.add)
+            else:
+                nc.vector.tensor_scalar(result[:], capped[t][:, slots], CAP, None, ALU.mult)
             nc.sync.dma_start(out_rows[:, t, slots], result[:])
 
         banks = ["score0", "score1", "score2", "score3", "turned0", "turned1", "wide0", "wide1"]

@@ -125,6 +125,33 @@ def tile_attend_link_budget_topk_kernel(tc, qT, k_words, k_scales, pr, pw, offs,
         out_rows = out[0].rearrange("(p t) n -> p t n", t=TILES)
         capped = [sb.tile([P, N], F32, name=f"capped{t}") for t in range(TILES)]
 
+        def product(t, slots, bank):
+            score = ps.tile([P, slots.stop - slots.start], F32, name=f"score{t}_{slots.start}", tag=bank)
+            nc.tensor.matmul_mx(
+                out=score[:],
+                lhsT=q_codes[:, t * P : (t + 1) * P].bitcast(FP8X4),
+                lhsT_scale=q_scales[:, t * P : (t + 1) * P],
+                rhs=g_words[:, slots].bitcast(FP8X4),
+                rhs_scale=g_scales[:, slots],
+                start=True,
+                stop=True,
+            )
+            return score
+
+        def cap(t, slots, score):
+            h, first = divmod(slots.start, NH)
+            width = slots.stop - slots.start
+            deficit = sb.tile([P, width], F32, name=f"deficit{t}_{slots.start}")
+            nc.vector.scalar_tensor_tensor(
+                deficit[:],
+                spread[h][:, first : first + width],
+                weight[:, t : t + 1],
+                score,
+                ALU.mult,
+                ALU.subtract,
+            )
+            nc.scalar.activation(capped[t][:, slots], deficit[:], ACT.Tanh, scale=-1.0 / CAP)
+
         def finish(t, slots):
             result = sb.tile([P, slots.stop - slots.start], F32, name=f"result{t}_{slots.start}")
             if t == 0 and slots.start == 0:
@@ -133,34 +160,21 @@ def tile_attend_link_budget_topk_kernel(tc, qT, k_words, k_scales, pr, pw, offs,
                 nc.vector.tensor_scalar(result[:], capped[t][:, slots], CAP, None, ALU.mult)
             nc.sync.dma_start(out_rows[:, t, slots], result[:])
 
-        banks = ["score0", "score1", "score2", "score3", "turned0", "turned1", "wide0", "wide1"]
-        for h in range(HALVES):
-            for t in range(TILES):
-                last = (h, t) in ((0, 0), (HALVES - 1, TILES - 1))
-                for c in range(blocks):
-                    slots = slice(h * NH + c * P, h * NH + (c + 1) * P)
-                    i = (h * TILES + t) * blocks + c
-                    score = ps.tile([P, P], F32, name=f"score{i}", tag=banks[i])
-                    nc.tensor.matmul_mx(
-                        out=score[:],
-                        lhsT=q_codes[:, t * P : (t + 1) * P].bitcast(FP8X4),
-                        lhsT_scale=q_scales[:, t * P : (t + 1) * P],
-                        rhs=g_words[:, slots].bitcast(FP8X4),
-                        rhs_scale=g_scales[:, slots],
-                        start=True,
-                        stop=True,
-                    )
-                    deficit = sb.tile([P, P], F32, name=f"deficit{i}")
-                    nc.vector.scalar_tensor_tensor(
-                        deficit[:],
-                        spread[h][:, c * P : (c + 1) * P],
-                        weight[:, t : t + 1],
-                        score[:],
-                        ALU.mult,
-                        ALU.subtract,
-                    )
-                    nc.scalar.activation(capped[t][:, slots], deficit[:], ACT.Tanh, scale=-1.0 / CAP)
-                    if last:
-                        finish(t, slots)
-                if not last:
-                    finish(t, slice(h * NH, (h + 1) * NH))
+        small = P // 2
+        for slots, bank in ((slice(0, small), "score0"), (slice(small, P), "score1")):
+            cap(0, slots, product(0, slots, bank)[:])
+        finish(0, slice(0, P))
+        banks = ["score2", "score3", "turned0", "turned1", "wide0", "wide1", "score0"]
+        rest = [(h, t, c) for h in range(HALVES) for t in range(TILES) for c in range(blocks)][1:]
+        for (h, t, c), bank in zip(rest[:-1], banks):
+            slots = slice(h * NH + c * P, h * NH + (c + 1) * P)
+            cap(t, slots, product(t, slots, bank)[:])
+            if (h, t) == (0, 0):
+                finish(t, slots)
+            elif c == blocks - 1:
+                finish(t, slice(h * NH, (h + 1) * NH))
+        score = product(TILES - 1, slice(N - P, N), banks[-1])
+        cap(TILES - 1, slice(N - P, N - small), score[:, :small])
+        finish(TILES - 1, slice(N - NH, N - small))
+        cap(TILES - 1, slice(N - small, N), score[:, small:])
+        finish(TILES - 1, slice(N - small, N))

@@ -166,15 +166,10 @@ def tile_attend_link_budget_topk_kernel(tc, qT, k_words, k_scales, pr, pw, offs,
         finish(0, slice(0, P))
         banks = ["score2", "score3", "turned0", "turned1", "wide0", "wide1", "score0"]
         rest = [(h, t, c) for h in range(HALVES) for t in range(TILES) for c in range(blocks)][1:]
-        for (h, t, c), bank in zip(rest[:-1], banks):
+        for (h, t, c), bank in zip(rest, banks):
             slots = slice(h * NH + c * P, h * NH + (c + 1) * P)
             cap(t, slots, product(t, slots, bank)[:])
             if (h, t) == (0, 0):
                 finish(t, slots)
             elif c == blocks - 1:
                 finish(t, slice(h * NH, (h + 1) * NH))
-        score = product(TILES - 1, slice(N - P, N), banks[-1])
-        cap(TILES - 1, slice(N - P, N - small), score[:, :small])
-        finish(TILES - 1, slice(N - NH, N - small))
-        cap(TILES - 1, slice(N - small, N), score[:, small:])
-        finish(TILES - 1, slice(N - small, N))

@@ -152,24 +152,30 @@ def tile_attend_link_budget_topk_kernel(tc, qT, k_words, k_scales, pr, pw, offs,
             )
             nc.scalar.activation(capped[t][:, slots], deficit[:], ACT.Tanh, scale=-1.0 / CAP)
 
-        def finish(t, slots):
+        def finish(t, slots, parts):
             result = sb.tile([P, slots.stop - slots.start], F32, name=f"result{t}_{slots.start}")
-            if t == 0 and slots.start == 0:
-                nc.gpsimd.tensor_scalar(result[:], capped[t][:, slots], CAP, 0.0, ALU.mult, ALU.add)
-            else:
-                nc.vector.tensor_scalar(result[:], capped[t][:, slots], CAP, None, ALU.mult)
+            for part in parts:
+                if t == 0 and slots.start == 0:
+                    nc.gpsimd.tensor_scalar(result[:, part], capped[t][:, slots][:, part], CAP, 0.0, ALU.mult, ALU.add)
+                else:
+                    nc.vector.tensor_scalar(result[:, part], capped[t][:, slots][:, part], CAP, None, ALU.mult)
             nc.sync.dma_start(out_rows[:, t, slots], result[:])
 
         small = P // 2
-        for slots, bank in ((slice(0, small), "score0"), (slice(small, P), "score1")):
-            cap(0, slots, product(0, slots, bank)[:])
-        finish(0, slice(0, P))
-        banks = ["score2", "score3", "turned0", "turned1", "wide0", "wide1", "score0"]
+        score = product(0, slice(0, P), "score0")
+        cap(0, slice(0, small), score[:, :small])
+        cap(0, slice(small, P), score[:, small:])
+        finish(0, slice(0, P), [slice(0, P)])
+        banks = ["score1", "score2", "score3", "turned0", "turned1", "wide0", "wide1"]
         rest = [(h, t, c) for h in range(HALVES) for t in range(TILES) for c in range(blocks)][1:]
-        for (h, t, c), bank in zip(rest, banks):
+        for (h, t, c), bank in zip(rest[:-1], banks):
             slots = slice(h * NH + c * P, h * NH + (c + 1) * P)
             cap(t, slots, product(t, slots, bank)[:])
             if (h, t) == (0, 0):
-                finish(t, slots)
+                finish(t, slots, [slice(0, P)])
             elif c == blocks - 1:
-                finish(t, slice(h * NH, (h + 1) * NH))
+                finish(t, slice(h * NH, (h + 1) * NH), [slice(0, NH)])
+        score = product(TILES - 1, slice(N - P, N), banks[-1])
+        cap(TILES - 1, slice(N - P, N - small), score[:, :small])
+        cap(TILES - 1, slice(N - small, N), score[:, small:])
+        finish(1, slice(NH, N), [slice(0, NH - small), slice(NH - small, NH)])

@@ -165,14 +165,14 @@ def tile_attend_link_budget_topk_kernel(tc, qT, k_words, k_scales, pr, pw, offs,
         score = product(0, slice(0, P), "score0")
         cap(0, slice(0, small), score[:, :small])
         cap(0, slice(small, P), score[:, small:])
-        finish(0, slice(0, P), [slice(0, P)])
+        finish(0, slice(0, small), [slice(0, small)])
         banks = ["score1", "score2", "score3", "turned0", "turned1", "wide0", "wide1"]
         rest = [(h, t, c) for h in range(HALVES) for t in range(TILES) for c in range(blocks)][1:]
         for (h, t, c), bank in zip(rest[:-1], banks):
             slots = slice(h * NH + c * P, h * NH + (c + 1) * P)
             cap(t, slots, product(t, slots, bank)[:])
             if (h, t) == (0, 0):
-                finish(t, slots, [slice(0, P)])
+                finish(t, slice(small, NH), [slice(0, NH - small)])
             elif c == blocks - 1:
                 finish(t, slice(h * NH, (h + 1) * NH), [slice(0, NH)])
         score = product(TILES - 1, slice(N - P, N), banks[-1])

@@ -25,7 +25,7 @@ SCALE_ROW = 48
 PRICES_AT = T
 WORDS_AT = PRICES_AT + 4 * T
 WEIGHT_AT = WORDS_AT + 4 * T
-PLANE_AT = WEIGHT_AT + 64
+PLANE_AT = WEIGHT_AT + 256
 
 FLOPS = 2 * D * NQ * N
 BYTES = 4 * D * NQ + D * T + 16 * T + 4 * T + 4 * NQ + 2 * N + 4 * NQ * N
@@ -40,7 +40,7 @@ def tile_attend_link_budget_topk_kernel(tc, qT, k_words, k_scales, pr, pw, offs,
 
         offsets = sb.tile([P, N // 16], U16, name="offsets")
         nc.sync.dma_start(offsets[:], offs)
-        scales = placed.tile([P, T], U8, name="scales", align_bytes=64, offset=0)
+        scales = placed.tile([P, T], U8, name="scales", align_bytes=256, offset=0)
         scale_words = scales[:].bitcast(I32)
         for rows in (slice(0, SCALE_ROW), slice(SCALE_ROW + 16, P)):
             nc.vector.memset(scale_words[rows, : T // 8 - 1], 0)
@@ -58,22 +58,22 @@ def tile_attend_link_budget_topk_kernel(tc, qT, k_words, k_scales, pr, pw, offs,
             pattern=[[-1, P]],
             channel_multiplier=1,
         )
-        prices = placed.tile([P, T], F32, name="prices", align_bytes=64, offset=PRICES_AT)
+        prices = placed.tile([P, T], F32, name="prices", align_bytes=256, offset=PRICES_AT)
         nc.vector.memset(prices[:PRICE_ROW, : CLEAR_V // 2 - 1], 0.0)
         nc.vector.memset(prices[:PRICE_ROW, CLEAR_V // 2 - 1 : CLEAR_V], 0.0)
         nc.gpsimd.memset(prices[:PRICE_ROW, CLEAR_V : CLEAR_V + P], 0.0)
         nc.gpsimd.memset(prices[:PRICE_ROW, CLEAR_V + P :], 0.0)
         nc.scalar.dma_start(prices[PRICE_ROW:, :], pr[PRICE_ROW:, :])
-        q_raw = sb.tile([P, PACK, NQ], F32, name="q_raw", tag="q_raw")
+        q_raw = sb.tile([P, PACK, NQ], F32, name="q_raw", tag="q_raw", align_bytes=256)
         nc.sync.dma_start(q_raw[:], qT[0].rearrange("(p j) q -> p j q", j=PACK))
-        words = placed.tile([P, T], I32, name="words", align_bytes=64, offset=WORDS_AT)
+        words = placed.tile([P, T], I32, name="words", align_bytes=256, offset=WORDS_AT)
         nc.sync.dma_start(words[:], k_words[0].rearrange("p t r -> p (t r)").bitcast(I32))
         weight = placed.tile([P, TILES], F32, name="weight", align_bytes=64, offset=WEIGHT_AT)
         nc.sync.dma_start(weight[:], pw[0].rearrange("(p t) o -> p (t o)", t=TILES))
 
-        g_rows = sb.tile([P, N], U8, name="g_rows", align_bytes=64)
+        g_rows = sb.tile([P, N], U8, name="g_rows", align_bytes=256)
         nc.vector.tensor_copy(g_rows[:], scales[:].indirect(offsets[:]))
-        g_scales = placed.tile([P, N], U8, name="g_scales", align_bytes=64, offset=PLANE_AT)
+        g_scales = placed.tile([P, N], U8, name="g_scales", align_bytes=256, offset=PLANE_AT)
         for quad in range(4):
             first = SCALE_ROW + 4 * quad
             nc.sync.dma_start(
@@ -89,7 +89,7 @@ def tile_attend_link_budget_topk_kernel(tc, qT, k_words, k_scales, pr, pw, offs,
 
         cols = NH // 16
         blocks = NH // P
-        columns = sb.tile([P, HALVES, blocks], F32, name="columns", tag="q_raw")
+        columns = sb.tile([P, HALVES, blocks], F32, name="columns", tag="q_raw", align_bytes=256)
         spread = []
         for h in range(HALVES):
             g_price = sb.tile([P, NH], F32, name=f"g_price{h}", align_bytes=64)
@@ -153,7 +153,7 @@ def tile_attend_link_budget_topk_kernel(tc, qT, k_words, k_scales, pr, pw, offs,
             nc.scalar.activation(capped[t][:, slots], deficit[:], ACT.Tanh, scale=-1.0 / CAP)
 
         def finish(t, slots, parts):
-            result = sb.tile([P, slots.stop - slots.start], F32, name=f"result{t}_{slots.start}")
+            result = sb.tile([P, slots.stop - slots.start], F32, name=f"result{t}_{slots.start}", align_bytes=256)
             for part in parts:
                 if t == 0 and slots.start == 0:
                     nc.gpsimd.tensor_scalar(result[:, part], capped[t][:, slots][:, part], CAP, 0.0, ALU.mult, ALU.add)

@@ -23,9 +23,9 @@ PRICE_ROW = P - 1
 CLEAR_V = 640
 SCALE_ROW = 48
 PRICES_AT = T
-WORDS_AT = PRICES_AT + 4 * T
-WEIGHT_AT = WORDS_AT + 4 * T
-PLANE_AT = WEIGHT_AT + 256
+PLANE_AT = PRICES_AT + 4 * T
+WEIGHT_AT = PLANE_AT + N
+WORDS_AT = WEIGHT_AT + 256
 
 FLOPS = 2 * D * NQ * N
 BYTES = 4 * D * NQ + D * T + 16 * T + 4 * T + 4 * NQ + 2 * N + 4 * NQ * N
@@ -46,7 +46,7 @@ def tile_attend_link_budget_topk_kernel(tc, qT, k_words, k_scales, pr, pw, offs,
             nc.vector.memset(scale_words[rows, : T // 8 - 1], 0)
             nc.vector.memset(scale_words[rows, T // 8 - 1 :], 0)
         nc.scalar.dma_start(scale_words[SCALE_ROW : SCALE_ROW + 16, :], k_scales[0].bitcast(I32))
-        zeros = placed.tile([P, P], F32, name="zeros", align_bytes=64, offset=WEIGHT_AT - 2 * P)
+        zeros = placed.tile([P, P], F32, name="zeros", align_bytes=64, offset=WEIGHT_AT - P)
         nc.gpsimd.memset(zeros[:], 0.0)
         ident = sb.tile([P, P], F32, name="ident")
         nc.gpsimd.affine_select(

@@ -48,9 +48,9 @@ def tile_attend_link_budget_topk_kernel(tc, qT, k_words, k_scales, pr, pw, offs,
         nc.scalar.dma_start(scale_words[SCALE_ROW : SCALE_ROW + 16, :], k_scales[0].bitcast(I32))
         zeros = placed.tile([P, P], F32, name="zeros", align_bytes=64, offset=WEIGHT_AT - P)
         nc.gpsimd.memset(zeros[:], 0.0)
-        ident = sb.tile([P, P], F32, name="ident")
+        diagonal = sb.tile([P, P], F32, name="diagonal", tag="g_price", align_bytes=64)
         nc.gpsimd.affine_select(
-            out=ident[:],
+            out=diagonal[:],
             in_=zeros[:],
             compare_op=ALU.not_equal,
             fill=1.0,
@@ -58,13 +58,15 @@ def tile_attend_link_budget_topk_kernel(tc, qT, k_words, k_scales, pr, pw, offs,
             pattern=[[-1, P]],
             channel_multiplier=1,
         )
+        ident = sb.tile([P, P], F32, name="ident")
+        nc.scalar.copy(ident[:], diagonal[:])
         prices = placed.tile([P, T], F32, name="prices", align_bytes=256, offset=PRICES_AT)
         nc.vector.memset(prices[:PRICE_ROW, : CLEAR_V // 2 - 1], 0.0)
         nc.vector.memset(prices[:PRICE_ROW, CLEAR_V // 2 - 1 : CLEAR_V], 0.0)
         nc.gpsimd.memset(prices[:PRICE_ROW, CLEAR_V : CLEAR_V + P], 0.0)
         nc.gpsimd.memset(prices[:PRICE_ROW, CLEAR_V + P :], 0.0)
-        nc.scalar.dma_start(prices[PRICE_ROW:, :], pr[PRICE_ROW:, :])
-        q_raw = sb.tile([P, PACK, NQ], F32, name="q_raw", tag="q_raw", align_bytes=256)
+        nc.sync.dma_start(prices[PRICE_ROW:, :], pr[PRICE_ROW:, :])
+        q_raw = sb.tile([P, PACK, NQ], F32, name="q_raw", align_bytes=256)
         nc.sync.dma_start(q_raw[:], qT[0].rearrange("(p j) q -> p j q", j=PACK))
         words = placed.tile([P, T], I32, name="words", align_bytes=256, offset=WORDS_AT)
         nc.sync.dma_start(words[:], k_words[0].rearrange("p t r -> p (t r)").bitcast(I32))
@@ -81,22 +83,24 @@ def tile_attend_link_budget_topk_kernel(tc, qT, k_words, k_scales, pr, pw, offs,
                 g_rows[first : first + 4, :].bitcast(I32),
             )
 
-        q_bf = sb.tile([P, TILES, P, PACK], BF16, name="q_bf", align_bytes=64)
-        nc.scalar.copy(
+        q_bf = placed.tile([P, TILES, P, PACK], BF16, name="q_bf", align_bytes=256, offset=0)
+        nc.vector.tensor_copy(
             q_bf[:].rearrange("p t (a m) j -> p a t m j", m=2),
             q_raw[:].rearrange("p j (a m t) -> p a t m j", m=2, t=TILES),
         )
 
         cols = NH // 16
         blocks = NH // P
-        columns = sb.tile([P, HALVES, blocks], F32, name="columns", tag="q_raw", align_bytes=256)
+        columns = sb.tile([P, HALVES, blocks], F32, name="columns")
+        g_price = sb.tile([P, N], F32, name="g_price", tag="g_price", align_bytes=64)
+        for h in range(HALVES):
+            listed = prices[:].indirect(offsets[:, h * cols : (h + 1) * cols])
+            nc.scalar.activation(g_price[:, h * NH : (h + 1) * NH], listed, ACT.Copy)
         spread = []
         for h in range(HALVES):
-            g_price = sb.tile([P, NH], F32, name=f"g_price{h}", align_bytes=64)
-            nc.vector.tensor_copy(g_price[:], prices[:].indirect(offsets[:, h * cols : (h + 1) * cols]))
             turned = ps.tile([P, blocks, P], F32, name=f"turned{h}", tag=f"turned{h}")
             for c in range(blocks):
-                nc.tensor.transpose(turned[:, c, :], g_price[:, c * P : (c + 1) * P], ident[:])
+                nc.tensor.transpose(turned[:, c, :], g_price[:, h * NH + c * P : h * NH + (c + 1) * P], ident[:])
             column = columns[:, h, :]
             nc.scalar.copy(column, turned[:, :, PRICE_ROW])
             wide = ps.tile([P, blocks, P], F32, name=f"wide{h}", tag=f"wide{h}")
@@ -115,7 +119,7 @@ def tile_attend_link_budget_topk_kernel(tc, qT, k_words, k_scales, pr, pw, offs,
             in_=q_bf[:].rearrange("p t m j -> p (t m j)"),
         )
 
-        g_words = placed.tile([P, N], U32, name="g_words", align_bytes=64, offset=0)
+        g_words = placed.tile([P, N], U32, name="g_words", align_bytes=256, offset=PRICES_AT + 4 * NQ)
         for h in range(HALVES):
             nc.vector.tensor_copy(
                 g_words[:, h * NH : (h + 1) * NH],

@@ -65,7 +65,7 @@ def tile_attend_link_budget_topk_kernel(tc, qT, k_words, k_scales, pr, pw, offs,
         nc.vector.memset(prices[:PRICE_ROW, CLEAR_V // 2 - 1 : CLEAR_V], 0.0)
         nc.gpsimd.memset(prices[:PRICE_ROW, CLEAR_V : CLEAR_V + P], 0.0)
         nc.gpsimd.memset(prices[:PRICE_ROW, CLEAR_V + P :], 0.0)
-        nc.sync.dma_start(prices[PRICE_ROW:, :], pr[PRICE_ROW:, :])
+        nc.scalar.dma_start(prices[PRICE_ROW:, :], pr[PRICE_ROW:, :])
         q_raw = sb.tile([P, PACK, NQ], F32, name="q_raw", align_bytes=256)
         nc.sync.dma_start(q_raw[:], qT[0].rearrange("(p j) q -> p j q", j=PACK))
         words = placed.tile([P, T], I32, name="words", align_bytes=256, offset=WORDS_AT)
@@ -83,30 +83,36 @@ def tile_attend_link_budget_topk_kernel(tc, qT, k_words, k_scales, pr, pw, offs,
                 g_rows[first : first + 4, :].bitcast(I32),
             )
 
+        cols = NH // 16
+        early = sb.tile([P, N - P], F32, name="g_price0", tag="g_price", align_bytes=64)
+        nc.scalar.activation(early[:, :NH], prices[:].indirect(offsets[:, :cols]), ACT.Copy)
+        nc.scalar.activation(early[:, NH:], prices[:].indirect(offsets[:, cols : 3 * cols // 2]), ACT.Copy)
+        last = sb.tile([P, P], F32, name="g_price1", align_bytes=64)
+        nc.vector.tensor_copy(last[:], prices[:].indirect(offsets[:, 3 * cols // 2 :]))
+        picked = [early[:, :P], early[:, P:NH], early[:, NH:], last[:]]
+
         q_bf = placed.tile([P, TILES, P, PACK], BF16, name="q_bf", align_bytes=256, offset=0)
         nc.vector.tensor_copy(
             q_bf[:].rearrange("p t (a m) j -> p a t m j", m=2),
             q_raw[:].rearrange("p j (a m t) -> p a t m j", m=2, t=TILES),
         )
 
-        cols = NH // 16
         blocks = NH // P
-        columns = sb.tile([P, HALVES, blocks], F32, name="columns")
-        g_price = sb.tile([P, N], F32, name="g_price", tag="g_price", align_bytes=64)
-        for h in range(HALVES):
-            listed = prices[:].indirect(offsets[:, h * cols : (h + 1) * cols])
-            nc.scalar.activation(g_price[:, h * NH : (h + 1) * NH], listed, ACT.Copy)
+
         spread = []
+        wides = []
         for h in range(HALVES):
             turned = ps.tile([P, blocks, P], F32, name=f"turned{h}", tag=f"turned{h}")
             for c in range(blocks):
-                nc.tensor.transpose(turned[:, c, :], g_price[:, h * NH + c * P : h * NH + (c + 1) * P], ident[:])
-            column = columns[:, h, :]
-            nc.scalar.copy(column, turned[:, :, PRICE_ROW])
+                nc.tensor.transpose(turned[:, c, :], picked[h * blocks + c], ident[:])
+            column = sb.tile([P, blocks], F32, name=f"column{h}", tag=f"column{h}")
+            nc.scalar.copy(column[:], turned[:, :, PRICE_ROW])
             wide = ps.tile([P, blocks, P], F32, name=f"wide{h}", tag=f"wide{h}")
             for c in range(blocks):
                 nc.tensor.transpose(wide[:, c, :], column[:, c : c + 1].to_broadcast([P, P]), ident[:])
-            price = sb.tile([P, NH], F32, name=f"price{h}")
+            wides.append(wide)
+        for h, wide in enumerate(wides):
+            price = sb.tile([P, NH], F32, name=f"price{h}", tag=f"column{1 - h}")
             nc.scalar.copy(price[:], wide[:].rearrange("p c n -> p (c n)"))
             spread.append(price)
 

from contextlib import ExitStack

import concourse.mybir as mybir

F32 = mybir.dt.float32
BF16 = mybir.dt.bfloat16
I32 = mybir.dt.int32
U32 = mybir.dt.uint32
U16 = mybir.dt.uint16
U8 = mybir.dt.uint8
FP8X4 = mybir.dt.float8_e4m3fn_x4
ALU = mybir.AluOpType
ACT = mybir.ActivationFunctionType

P = 128
D, NQ, T, N = 512, 256, 2048, 512
PACK = 4
TILES = NQ // P
HALVES = 2
NH = N // HALVES
CAP = 10.0
PRICE_ROW = P - 1
CLEAR_V = 640
SCALE_ROW = 48
PRICES_AT = T
PLANE_AT = PRICES_AT + 4 * T
WEIGHT_AT = PLANE_AT + N
WORDS_AT = WEIGHT_AT + 256

FLOPS = 2 * D * NQ * N
BYTES = 4 * D * NQ + D * T + 16 * T + 4 * T + 4 * NQ + 2 * N + 4 * NQ * N


def tile_attend_link_budget_topk_kernel(tc, qT, k_words, k_scales, pr, pw, offs, out):
    nc = tc.nc
    with ExitStack() as ctx:
        sb = ctx.enter_context(tc.tile_pool(name="sb", bufs=1))
        placed = ctx.enter_context(tc.tile_pool(name="placed", bufs=1))
        ps = ctx.enter_context(tc.psum_pool(name="ps", bufs=1))

        offsets = sb.tile([P, N // 16], U16, name="offsets")
        nc.sync.dma_start(offsets[:], offs)
        scales = placed.tile([P, T], U8, name="scales", align_bytes=256, offset=0)
        scale_words = scales[:].bitcast(I32)
        for rows in (slice(0, SCALE_ROW), slice(SCALE_ROW + 16, P)):
            nc.vector.memset(scale_words[rows, : T // 8 - 1], 0)
            nc.vector.memset(scale_words[rows, T // 8 - 1 :], 0)
        nc.scalar.dma_start(scale_words[SCALE_ROW : SCALE_ROW + 16, :], k_scales[0].bitcast(I32))
        zeros = placed.tile([P, P], F32, name="zeros", align_bytes=64, offset=WEIGHT_AT - P)
        nc.gpsimd.memset(zeros[:], 0.0)
        diagonal = sb.tile([P, P], F32, name="diagonal", tag="g_price", align_bytes=64)
        nc.gpsimd.affine_select(
            out=diagonal[:],
            in_=zeros[:],
            compare_op=ALU.not_equal,
            fill=1.0,
            base=0,
            pattern=[[-1, P]],
            channel_multiplier=1,
        )
        ident = sb.tile([P, P], F32, name="ident")
        nc.scalar.copy(ident[:], diagonal[:])
        prices = placed.tile([P, T], F32, name="prices", align_bytes=256, offset=PRICES_AT)
        nc.vector.memset(prices[:PRICE_ROW, : CLEAR_V // 2 - 1], 0.0)
        nc.vector.memset(prices[:PRICE_ROW, CLEAR_V // 2 - 1 : CLEAR_V], 0.0)
        nc.gpsimd.memset(prices[:PRICE_ROW, CLEAR_V : CLEAR_V + P], 0.0)
        nc.gpsimd.memset(prices[:PRICE_ROW, CLEAR_V + P :], 0.0)
        nc.scalar.dma_start(prices[PRICE_ROW:, :], pr[PRICE_ROW:, :])
        q_raw = sb.tile([P, PACK, NQ], F32, name="q_raw", align_bytes=256)
        nc.sync.dma_start(q_raw[:], qT[0].rearrange("(p j) q -> p j q", j=PACK))
        words = placed.tile([P, T], I32, name="words", align_bytes=256, offset=WORDS_AT)
        nc.sync.dma_start(words[:], k_words[0].rearrange("p t r -> p (t r)").bitcast(I32))
        weight = placed.tile([P, TILES], F32, name="weight", align_bytes=64, offset=WEIGHT_AT)
        nc.sync.dma_start(weight[:], pw[0].rearrange("(p t) o -> p (t o)", t=TILES))

        g_rows = sb.tile([P, N], U8, name="g_rows", align_bytes=256)
        nc.vector.tensor_copy(g_rows[:], scales[:].indirect(offsets[:]))
        g_scales = placed.tile([P, N], U8, name="g_scales", align_bytes=256, offset=PLANE_AT)
        for quad in range(4):
            first = SCALE_ROW + 4 * quad
            nc.sync.dma_start(
                g_scales[32 * quad : 32 * quad + 4, :].bitcast(I32),
                g_rows[first : first + 4, :].bitcast(I32),
            )

        cols = NH // 16
        early = sb.tile([P, N - P], F32, name="g_price0", tag="g_price", align_bytes=64)
        nc.scalar.activation(early[:, :NH], prices[:].indirect(offsets[:, :cols]), ACT.Copy)
        nc.scalar.activation(early[:, NH:], prices[:].indirect(offsets[:, cols : 3 * cols // 2]), ACT.Copy)
        last = sb.tile([P, P], F32, name="g_price1", align_bytes=64)
        nc.vector.tensor_copy(last[:], prices[:].indirect(offsets[:, 3 * cols // 2 :]))
        picked = [early[:, :P], early[:, P:NH], early[:, NH:], last[:]]

        q_bf = placed.tile([P, TILES, P, PACK], BF16, name="q_bf", align_bytes=256, offset=0)
        nc.vector.tensor_copy(
            q_bf[:].rearrange("p t (a m) j -> p a t m j", m=2),
            q_raw[:].rearrange("p j (a m t) -> p a t m j", m=2, t=TILES),
        )

        blocks = NH // P

        spread = []
        wides = []
        for h in range(HALVES):
            turned = ps.tile([P, blocks, P], F32, name=f"turned{h}", tag=f"turned{h}")
            for c in range(blocks):
                nc.tensor.transpose(turned[:, c, :], picked[h * blocks + c], ident[:])
            column = sb.tile([P, blocks], F32, name=f"column{h}", tag=f"column{h}")
            nc.scalar.copy(column[:], turned[:, :, PRICE_ROW])
            wide = ps.tile([P, blocks, P], F32, name=f"wide{h}", tag=f"wide{h}")
            for c in range(blocks):
                nc.tensor.transpose(wide[:, c, :], column[:, c : c + 1].to_broadcast([P, P]), ident[:])
            wides.append(wide)
        for h, wide in enumerate(wides):
            price = sb.tile([P, NH], F32, name=f"price{h}", tag=f"column{1 - h}")
            nc.scalar.copy(price[:], wide[:].rearrange("p c n -> p (c n)"))
            spread.append(price)


        q_codes = placed.tile([P, NQ], U32, name="q_codes", align_bytes=64, offset=PRICES_AT)
        q_scales = sb.tile([P, NQ], U8, name="q_scales", align_bytes=64)
        nc.vector.quantize_mx(
            out=q_codes[:].bitcast(FP8X4),
            scales=q_scales[:],
            in_=q_bf[:].rearrange("p t m j -> p (t m j)"),
        )

        g_words = placed.tile([P, N], U32, name="g_words", align_bytes=256, offset=PRICES_AT + 4 * NQ)
        for h in range(HALVES):
            nc.vector.tensor_copy(
                g_words[:, h * NH : (h + 1) * NH],
                words[:].bitcast(U32).indirect(offsets[:, h * cols : (h + 1) * cols]),
            )

        out_rows = out[0].rearrange("(p t) n -> p t n", t=TILES)
        capped = [sb.tile([P, N], F32, name=f"capped{t}") for t in range(TILES)]

        def product(t, slots, bank):
            score = ps.tile([P, slots.stop - slots.start], F32, name=f"score{t}_{slots.start}", tag=bank)
            nc.tensor.matmul_mx(
                out=score[:],
                lhsT=q_codes[:, t * P : (t + 1) * P].bitcast(FP8X4),
                lhsT_scale=q_scales[:, t * P : (t + 1) * P],
                rhs=g_words[:, slots].bitcast(FP8X4),
                rhs_scale=g_scales[:, slots],
                start=True,
                stop=True,
            )
            return score

        def cap(t, slots, score):
            h, first = divmod(slots.start, NH)
            width = slots.stop - slots.start
            deficit = sb.tile([P, width], F32, name=f"deficit{t}_{slots.start}")
            nc.vector.scalar_tensor_tensor(
                deficit[:],
                spread[h][:, first : first + width],
                weight[:, t : t + 1],
                score,
                ALU.mult,
                ALU.subtract,
            )
            nc.scalar.activation(capped[t][:, slots], deficit[:], ACT.Tanh, scale=-1.0 / CAP)

        def finish(t, slots, parts):
            result = sb.tile([P, slots.stop - slots.start], F32, name=f"result{t}_{slots.start}", align_bytes=256)
            for part in parts:
                if t == 0 and slots.start == 0:
                    nc.gpsimd.tensor_scalar(result[:, part], capped[t][:, slots][:, part], CAP, 0.0, ALU.mult, ALU.add)
                else:
                    nc.vector.tensor_scalar(result[:, part], capped[t][:, slots][:, part], CAP, None, ALU.mult)
            nc.sync.dma_start(out_rows[:, t, slots], result[:])

        small = P // 2
        score = product(0, slice(0, P), "score0")
        cap(0, slice(0, small), score[:, :small])
        cap(0, slice(small, P), score[:, small:])
        finish(0, slice(0, small), [slice(0, small)])
        banks = ["score1", "score2", "score3", "turned0", "turned1", "wide0", "wide1"]
        rest = [(h, t, c) for h in range(HALVES) for t in range(TILES) for c in range(blocks)][1:]
        for (h, t, c), bank in zip(rest[:-1], banks):
            slots = slice(h * NH + c * P, h * NH + (c + 1) * P)
            cap(t, slots, product(t, slots, bank)[:])
            if (h, t) == (0, 0):
                finish(t, slice(small, NH), [slice(0, NH - small)])
            elif c == blocks - 1:
                finish(t, slice(h * NH, (h + 1) * NH), [slice(0, NH)])
        score = product(TILES - 1, slice(N - P, N), banks[-1])
        cap(TILES - 1, slice(N - P, N - small), score[:, :small])
        cap(TILES - 1, slice(N - small, N), score[:, small:])
        finish(1, slice(NH, N), [slice(0, NH - small), slice(NH - small, NH)])
